import numpy as np
CORES = [9,17,137,145,265,273,393,401]
N = 8
T = 128
def entries(a): return a.T.reshape(-1)
def pack(v, P): return np.ascontiguousarray(np.asarray(v, np.int32).reshape(-1, P).T)
def lists(rng, how):
    n = rng.integers(0, T + 1, N)
    if how == "none": n[rng.integers(N)] = 0; n[0] = 0
    if how == "full": n[:] = T
    if how == "one": n[:] = 1
    if how == "lone": z = int(rng.integers(N)); n[:] = 0; n[z] = int(rng.integers(1, T + 1))
    if how == "void": n[:] = 0
    return {"ln": np.broadcast_to(pack(np.concatenate([n, np.zeros(32 - N, np.int64)]), 16), (N, 16, 2)).copy()}
def setup_inputs(rng):
    return dict({"x": rng.standard_normal((N, 128, T), dtype=np.float32)}, **lists(rng, "uniform"))
def setup_inputs_full(rng):
    d = setup_inputs(rng); d.update(lists(rng, "full"))
    for k in ("x",): d[k] = (d[k].astype(np.float32) * 1048576.0).astype(d[k].dtype)
    return d
def setup_inputs_lone(rng):
    d = setup_inputs(rng); d.update(lists(rng, "lone"))
    for k in ("x",): d[k] = (d[k].astype(np.float32) * (1 / 1024.0)).astype(d[k].dtype)
    return d
def setup_inputs_none(rng):
    d = setup_inputs(rng); d.update(lists(rng, "none"))
    return d
def setup_inputs_one(rng):
    d = setup_inputs(rng); d.update(lists(rng, "one"))
    return d
def setup_inputs_void(rng):
    d = setup_inputs(rng); d.update(lists(rng, "void"))
    return d
def check_inputs(x):
    bad = []
    if x["ln"].min() < 0 or x["ln"].max() >= T + 1: bad.append("ln out of range")
    if entries(x["ln"][0])[N:].any(): bad.append("an entry from N on isn't 0")
    if not all(np.array_equal(a, x["ln"][0]) for a in x["ln"]): bad.append("ln isn't alike on all ranks")
    return bad
def reference(x, ln):
    n = entries(ln[0]); got = np.concatenate([x[r][:, :n[r]] for r in range(N)], axis=1)
    y = np.zeros((128, N * T), x.dtype); y[:, :got.shape[1]] = got
    return {"y": np.broadcast_to(y, (N, 128, N * T))}

@@ -1,0 +1,209 @@
+from concourse.bass import DstId, RemoteDMATransfer
+from concourse.mybir import AluOpType, ActivationFunctionType
+
+N = 8
+W = 128
+WORLD = 512
+ZC = N * W
+NP = 2
+PW = ZC // NP
+NE = 8
+
+SCRATCH = {
+    "win": ("sbuf", [128, ZC + 4], "float32"),
+    "outb": ("sbuf", [128, ZC], "float32"),
+    "hold": ("dram", [128, W], "float32"),
+    "lnrow": ("sbuf", [128, 16], "int32"),
+    "lnb": ("sbuf", [128, 16], "int32"),
+    "lnf": ("sbuf", [128, N], "float32"),
+    "cum": ("sbuf", [128, N], "float32"),
+    "gap": ("sbuf", [128, N], "float32"),
+    "zer": ("sbuf", [128, N], "float32"),
+    "pm": ("sbuf", [128, 1], "int32"),
+    "pmf": ("sbuf", [128, 1], "float32"),
+    "c16": ("sbuf", [128, 64], "float32"),
+    "c16w": ("sbuf", [128, 64], "float32"),
+    "jj": ("sbuf", [128, 64], "float32"),
+    "jw": ("sbuf", [128, 64], "float32"),
+    "tmp": ("sbuf", [128, 64 * N], "float32"),
+    "off": ("sbuf", [128, 64], "uint16"),
+}
+SEMAPHORES = (["a%d" % b for b in range(N)] + ["p%d" % q for q in range(NP)]
+              + ["fed", "sent", "ldd", "lnl", "gi", "gb", "vs", "zs", "offr", "sts", "sta"])
+
+_CACHE = {}
+
+
+def _low(mask, n):
+    out, bit, k = 0, 1, 0
+    while k < n:
+        assert bit <= mask
+        if mask & bit:
+            out |= bit
+            k += 1
+        bit <<= 1
+    return out
+
+
+def _plan(ranks, topo):
+    world = range(WORLD)
+    idx = dict((c, i) for i, c in enumerate(ranks))
+    calls, expect = {}, {}
+
+    def twin(s):
+        return [d for d in ranks if d != s and topo.host(d) == topo.host(s)][0]
+
+    def near(s):
+        return [d for d in ranks if topo.same_plane(s, d)][0]
+
+    def cabled(s):
+        return [d for d in ranks if topo.rack(topo.host(d)) != topo.rack(topo.host(s)) and topo.may_write(s, d)][0]
+
+    def gate(d, same_die):
+        return [x for x in world if topo.mates(x, d) and topo.may_write(x, d)
+                and (topo.die(x) == topo.die(d)) == same_die][0]
+
+    def porter(q):
+        return [x for x in world if x != q and topo.host(x) == topo.host(q) and topo.chip(x) == topo.chip(q)
+                and topo.may_write(x, twin(q)) and topo.die(x) != topo.die(q)][0]
+
+    def add(core, waits, src, sem, dsts):
+        calls.setdefault(core, []).append((waits, src, sem, dsts))
+        for d, _ in dsts:
+            assert topo.may_write(core, d) and d != core
+            expect[(d, sem)] = expect.get((d, sem), 0) + NE
+        expect[(core, "sent")] = expect.get((core, "sent"), 0) + NE
+
+    for s in ranks:
+        b = idx[s]
+        a = "a%d" % b
+        q = cabled(s)
+        far, g_own, g_near = porter(q), gate(twin(s), True), gate(twin(near(s)), False)
+        expect[(s, a)] = 16
+        expect[(s, "ldd")] = 16
+        add(s, ["ldd"], None, "fed", [(far, None), (g_near, None), (g_own, None)])
+        add(s, [], None, a, [(q, b), (near(s), b)])
+        add(far, ["fed"], None, a, [(twin(q), b), (twin(near(q)), b)])
+        add(g_near, ["fed"], None, a, [(twin(near(s)), b)])
+        add(g_own, ["fed"], None, a, [(twin(s), b)])
+    for s in ranks:
+        b = idx[cabled(s)]
+        add(s, ["a%d" % b], b, "a%d" % b, [(near(s), b)])
+    return calls, expect
+
+
+def _remote(g, core, T, topo, call, expect):
+    waits, src, sem, dsts = call
+
+    def ap(where):
+        return T.hold[:, :] if where is None else T.win[:, where * W:(where + 1) * W]
+
+    for name in waits:
+        g.wait_ge(T.sem[name], expect[(core, name)])
+    mask = topo.mask(core, dsts[0][0])
+    ids = []
+    for d, _ in dsts:
+        mask &= topo.mask(core, d)
+        rid, pid = topo.addr(d, core)
+        ids.append(DstId(rid=rid, pnc=pid))
+    g.remote_dma_fused([RemoteDMATransfer(dst_ids=ids, dma_engine_mask=_low(mask, NE), remote_sem=T.sem[sem],
+                                          srcs=[ap(src)], dsts=[ap(where) for _, where in dsts])],
+                       local_sem=T.sem.sent)
+
+
+def rank_program(g, core, T, topo):
+    if "plan" not in _CACHE:
+        _CACHE["plan"] = _plan(list(T.cores), topo)
+    calls, expect = _CACHE["plan"]
+    mine = calls.get(core, [])
+    rank = T.rank_of(core)
+    if rank is None:
+        for call in mine:
+            _remote(g, core, T, topo, call, expect)
+        if mine:
+            g.wait_ge(T.sem.sent, expect[(core, "sent")])
+        return
+
+    sem, v, act, add, mult = T.sem, g.vector, g.scalar, AluOpType.add, AluOpType.mult
+    own = T.win[:, rank * W:(rank + 1) * W]
+
+    g.sync.dma_start(out=T.hold[:, :], in_=T.x[:, :]).then_inc(sem.ldd, 16)
+    act.dma_start(out=T.lnrow[0:1, 0:16], in_=T.ln[0:8, :]).then_inc(sem.lnl, 16)
+    act.dma_start(out=own, in_=T.x[:, :]).then_inc(sem["a%d" % rank], 16)
+
+    g.iota(T.pm[:, 0:1], [[0, 1]], 0, 1).then_inc(sem.gi, 1)
+    g.iota(T.c16[:, :], [[16, 64]], 0, 0, allow_small_or_imprecise_dtypes=True).then_inc(sem.gi, 1)
+    g.iota(T.c16w[:, :], [[0, NP], [16, 64 // NP]], 0, 0,
+           allow_small_or_imprecise_dtypes=True).then_inc(sem.gi, 1)
+    _remote(g, core, T, topo, mine[0], expect)
+    _remote(g, core, T, topo, mine[1], expect)
+    g.wait_ge(sem.lnl, 16)
+    g.partition_broadcast(T.lnb[:, :], T.lnrow[0:1, 0:16], 128).then_inc(sem.gb, 1)
+    for call in mine[2:]:
+        _remote(g, core, T, topo, call, expect)
+    g.wait_ge(sem.sent, expect[(core, "sent")])
+
+    n = [0]
+
+    def done(inst):
+        inst.then_inc(sem.vs, 1)
+        n[0] += 1
+
+    def bar():
+        v.wait_ge(sem.vs, n[0])
+
+    v.memset(T.win[:, ZC:ZC + 4], 0.0).then_inc(sem.zs, 1)
+    done(v.memset(T.zer[:, :], 0.0))
+    v.wait_ge(sem.gi, 3)
+    done(v.tensor_scalar(out=T.pm[:, 0:1], in0=T.pm[:, 0:1], scalar1=15, scalar2=None, op0=AluOpType.bitwise_and))
+    bar()
+    done(v.tensor_copy(out=T.pmf[:, 0:1], in_=T.pm[:, 0:1]))
+    bar()
+    done(v.tensor_scalar(out=T.jj[:, :], in0=T.c16[:, :], scalar1=T.pmf[:, 0:1], scalar2=None, op0=add))
+    done(v.tensor_scalar(out=T.jw[:, :], in0=T.c16w[:, :], scalar1=T.pmf[:, 0:1], scalar2=None, op0=add))
+    v.wait_ge(sem.gb, 1)
+    done(v.tensor_copy(out=T.lnf[:, :], in_=T.lnb[:, 0:16:2]))
+    bar()
+    done(v.tensor_tensor_scan(out=T.cum[:, :], data0=T.lnf[:, :], data1=T.zer[:, :], initial=0.0, op0=add, op1=add))
+    done(v.tensor_scalar(out=T.gap[:, :], in0=T.lnf[:, :], scalar1=-1.0, scalar2=float(W), op0=mult, op1=add))
+    bar()
+    for r in range(N):
+        done(v.tensor_scalar(out=T.tmp[:, 64 * r:64 * (r + 1)], in0=T.jj[:, :], scalar1=T.cum[:, r:r + 1],
+                             scalar2=T.gap[:, r:r + 1], op0=AluOpType.is_ge, op1=mult))
+    bar()
+    h = 64 * N // 2
+    while h >= 64:
+        done(v.tensor_tensor(out=T.tmp[:, 0:h], in0=T.tmp[:, 0:h], in1=T.tmp[:, h:2 * h], op=add))
+        bar()
+        h //= 2
+    done(v.tensor_tensor(out=T.tmp[:, 0:64], in0=T.tmp[:, 0:64], in1=T.jw[:, :], op=add))
+    bar()
+    k = 64 // NP
+    for q in range(NP):
+        v.tensor_scalar(out=T.off[:, q * k:(q + 1) * k], in0=T.tmp[:, q * k:(q + 1) * k], scalar1=float(ZC - q * PW),
+                        scalar2=None, op0=AluOpType.min).then_inc(sem.offr, 1)
+
+    for eng in (v, act):
+        eng.wait_ge(sem.offr, NP)
+        eng.wait_ge(sem.zs, 1)
+    seen = {0: N, 1: N}
+    stores = {0: 0, 1: 0}
+    for q in range(NP - 1, -1, -1):
+        e = q % 2
+        eng = act if e else v
+        first = q * PW // W
+        for b in range(seen[e] - 1, first - 1, -1):
+            eng.wait_ge(sem["a%d" % b], expect[(core, "a%d" % b)])
+        seen[e] = first
+        src = T.win[:, q * PW:ZC + 4].indirect(T.off[:, q * k:(q + 1) * k])
+        dst = T.outb[:, q * PW:(q + 1) * PW]
+        if e:
+            act.activation(out=dst, in_=src, func=ActivationFunctionType.Copy).then_inc(sem["p%d" % q], 1)
+        else:
+            v.tensor_copy(out=dst, in_=src).then_inc(sem["p%d" % q], 1)
+        dq = act if e else g.sync
+        dq.wait_ge(sem["p%d" % q], 1)
+        dq.dma_start(out=T.y[:, q * PW:(q + 1) * PW], in_=dst).then_inc(sem.sta if e else sem.sts, 16)
+        stores[e] += 16
+    g.sync.wait_ge(sem.sts, stores[0])
+    act.wait_ge(sem.sta, stores[1])

@@ -5,7 +5,7 @@ N = 8
 W = 128
 WORLD = 512
 ZC = N * W
-NP = 2
+NP = 4
 PW = ZC // NP
 NE = 8
 
@@ -29,20 +29,15 @@ SCRATCH = {
     "off": ("sbuf", [128, 64], "uint16"),
 }
 SEMAPHORES = (["a%d" % b for b in range(N)] + ["p%d" % q for q in range(NP)]
-              + ["fed", "sent", "ldd", "lnl", "gi", "gb", "vs", "zs", "offr", "sts", "sta"])
+              + ["fed", "sent", "ldd", "lnl", "gi", "gb", "vs", "zs", "offr", "sts"])
 
 _CACHE = {}
 
 
-def _low(mask, n):
-    out, bit, k = 0, 1, 0
-    while k < n:
-        assert bit <= mask
-        if mask & bit:
-            out |= bit
-            k += 1
-        bit <<= 1
-    return out
+def _engines(mask, part):
+    bits = [1 << i for i in range(mask.bit_length()) if mask >> i & 1][:NE]
+    assert len(bits) == NE
+    return sum(bits if part is None else bits[part::2])
 
 
 def _plan(ranks, topo):
@@ -63,52 +58,51 @@ def _plan(ranks, topo):
         return [x for x in world if topo.mates(x, d) and topo.may_write(x, d)
                 and (topo.die(x) == topo.die(d)) == same_die][0]
 
-    def porter(q):
-        return [x for x in world if x != q and topo.host(x) == topo.host(q) and topo.chip(x) == topo.chip(q)
-                and topo.may_write(x, twin(q)) and topo.die(x) != topo.die(q)][0]
-
-    def add(core, waits, src, sem, dsts):
-        calls.setdefault(core, []).append((waits, src, sem, dsts))
-        for d, _ in dsts:
-            assert topo.may_write(core, d) and d != core
-            expect[(d, sem)] = expect.get((d, sem), 0) + NE
-        expect[(core, "sent")] = expect.get((core, "sent"), 0) + NE
+    def add(core, waits, transfers):
+        calls.setdefault(core, []).append((waits, transfers))
+        for _, sem, dsts, part in transfers:
+            ne = NE if part is None else NE // 2
+            for d, _ in dsts:
+                assert topo.may_write(core, d) and d != core
+                expect[(d, sem)] = expect.get((d, sem), 0) + ne
+            expect[(core, "sent")] = expect.get((core, "sent"), 0) + ne
 
     for s in ranks:
         b = idx[s]
         a = "a%d" % b
         q = cabled(s)
-        far, g_own, g_near = porter(q), gate(twin(s), True), gate(twin(near(s)), False)
+        g_own, g_near = gate(twin(s), True), gate(twin(near(s)), False)
         expect[(s, a)] = 16
         expect[(s, "ldd")] = 16
-        add(s, ["ldd"], None, "fed", [(far, None), (g_near, None), (g_own, None)])
-        add(s, [], None, a, [(q, b), (near(s), b)])
-        add(far, ["fed"], None, a, [(twin(q), b), (twin(near(q)), b)])
-        add(g_near, ["fed"], None, a, [(twin(near(s)), b)])
-        add(g_own, ["fed"], None, a, [(twin(s), b)])
+        add(s, ["ldd"], [(None, "fed", [(g_near, None), (g_own, None)], 1)])
+        add(s, [], [(None, a, [(q, b)], 0), (None, a, [(near(s), b)], 1)])
+        add(g_near, ["fed"], [(None, a, [(twin(near(q)), b)], 0), (None, a, [(twin(near(s)), b)], 1)])
+        add(g_own, ["fed"], [(None, a, [(twin(q), b)], 0), (None, a, [(twin(s), b)], 1)])
     for s in ranks:
         b = idx[cabled(s)]
-        add(s, ["a%d" % b], b, "a%d" % b, [(near(s), b)])
+        add(s, ["a%d" % b], [(b, "a%d" % b, [(near(s), b)], None)])
     return calls, expect
 
 
 def _remote(g, core, T, topo, call, expect):
-    waits, src, sem, dsts = call
+    waits, transfers = call
 
     def ap(where):
         return T.hold[:, :] if where is None else T.win[:, where * W:(where + 1) * W]
 
     for name in waits:
         g.wait_ge(T.sem[name], expect[(core, name)])
-    mask = topo.mask(core, dsts[0][0])
-    ids = []
-    for d, _ in dsts:
-        mask &= topo.mask(core, d)
-        rid, pid = topo.addr(d, core)
-        ids.append(DstId(rid=rid, pnc=pid))
-    g.remote_dma_fused([RemoteDMATransfer(dst_ids=ids, dma_engine_mask=_low(mask, NE), remote_sem=T.sem[sem],
-                                          srcs=[ap(src)], dsts=[ap(where) for _, where in dsts])],
-                       local_sem=T.sem.sent)
+    out = []
+    for src, sem, dsts, part in transfers:
+        mask = topo.mask(core, dsts[0][0])
+        ids = []
+        for d, _ in dsts:
+            mask &= topo.mask(core, d)
+            rid, pid = topo.addr(d, core)
+            ids.append(DstId(rid=rid, pnc=pid))
+        out.append(RemoteDMATransfer(dst_ids=ids, dma_engine_mask=_engines(mask, part), remote_sem=T.sem[sem],
+                                     srcs=[ap(src)], dsts=[ap(where) for _, where in dsts]))
+    g.remote_dma_fused(out, local_sem=T.sem.sent)
 
 
 def rank_program(g, core, T, topo):
@@ -135,8 +129,8 @@ def rank_program(g, core, T, topo):
     g.iota(T.c16[:, :], [[16, 64]], 0, 0, allow_small_or_imprecise_dtypes=True).then_inc(sem.gi, 1)
     g.iota(T.c16w[:, :], [[0, NP], [16, 64 // NP]], 0, 0,
            allow_small_or_imprecise_dtypes=True).then_inc(sem.gi, 1)
-    _remote(g, core, T, topo, mine[0], expect)
-    _remote(g, core, T, topo, mine[1], expect)
+    for call in mine[0:2]:
+        _remote(g, core, T, topo, call, expect)
     g.wait_ge(sem.lnl, 16)
     g.partition_broadcast(T.lnb[:, :], T.lnrow[0:1, 0:16], 128).then_inc(sem.gb, 1)
     for call in mine[2:]:
@@ -187,7 +181,6 @@ def rank_program(g, core, T, topo):
         eng.wait_ge(sem.offr, NP)
         eng.wait_ge(sem.zs, 1)
     seen = {0: N, 1: N}
-    stores = {0: 0, 1: 0}
     for q in range(NP - 1, -1, -1):
         e = q % 2
         eng = act if e else v
@@ -201,9 +194,9 @@ def rank_program(g, core, T, topo):
             act.activation(out=dst, in_=src, func=ActivationFunctionType.Copy).then_inc(sem["p%d" % q], 1)
         else:
             v.tensor_copy(out=dst, in_=src).then_inc(sem["p%d" % q], 1)
-        dq = act if e else g.sync
-        dq.wait_ge(sem["p%d" % q], 1)
-        dq.dma_start(out=T.y[:, q * PW:(q + 1) * PW], in_=dst).then_inc(sem.sta if e else sem.sts, 16)
-        stores[e] += 16
-    g.sync.wait_ge(sem.sts, stores[0])
-    act.wait_ge(sem.sta, stores[1])
+
+    for q in range(NP - 2, -1, -2):
+        g.sync.wait_ge(sem["p%d" % (q + 1)], 1)
+        g.sync.wait_ge(sem["p%d" % q], 1)
+        g.sync.dma_start(out=T.y[:, q * PW:(q + 2) * PW], in_=T.outb[:, q * PW:(q + 2) * PW]).then_inc(sem.sts, 16)
+    g.sync.wait_ge(sem.sts, 16 * (NP // 2))

from concourse.bass import DstId, RemoteDMATransfer
from concourse.mybir import AluOpType, ActivationFunctionType

N = 8
W = 128
WORLD = 512
ZC = N * W
NP = 4
PW = ZC // NP
NE = 8

SCRATCH = {
    "win": ("sbuf", [128, ZC + 4], "float32"),
    "outb": ("sbuf", [128, ZC], "float32"),
    "hold": ("dram", [128, W], "float32"),
    "lnrow": ("sbuf", [128, 16], "int32"),
    "lnb": ("sbuf", [128, 16], "int32"),
    "lnf": ("sbuf", [128, N], "float32"),
    "cum": ("sbuf", [128, N], "float32"),
    "gap": ("sbuf", [128, N], "float32"),
    "zer": ("sbuf", [128, N], "float32"),
    "pm": ("sbuf", [128, 1], "int32"),
    "pmf": ("sbuf", [128, 1], "float32"),
    "c16": ("sbuf", [128, 64], "float32"),
    "c16w": ("sbuf", [128, 64], "float32"),
    "jj": ("sbuf", [128, 64], "float32"),
    "jw": ("sbuf", [128, 64], "float32"),
    "tmp": ("sbuf", [128, 64 * N], "float32"),
    "off": ("sbuf", [128, 64], "uint16"),
}
SEMAPHORES = (["a%d" % b for b in range(N)] + ["p%d" % q for q in range(NP)]
              + ["fed", "sent", "ldd", "lnl", "gi", "gb", "vs", "zs", "offr", "sts"])

_CACHE = {}


def _engines(mask, part):
    bits = [1 << i for i in range(mask.bit_length()) if mask >> i & 1][:NE]
    assert len(bits) == NE
    return sum(bits if part is None else bits[part::2])


def _plan(ranks, topo):
    world = range(WORLD)
    idx = dict((c, i) for i, c in enumerate(ranks))
    calls, expect = {}, {}

    def twin(s):
        return [d for d in ranks if d != s and topo.host(d) == topo.host(s)][0]

    def near(s):
        return [d for d in ranks if topo.same_plane(s, d)][0]

    def cabled(s):
        return [d for d in ranks if topo.rack(topo.host(d)) != topo.rack(topo.host(s)) and topo.may_write(s, d)][0]

    def gate(d, same_die):
        return [x for x in world if topo.mates(x, d) and topo.may_write(x, d)
                and (topo.die(x) == topo.die(d)) == same_die][0]

    def add(core, waits, transfers):
        calls.setdefault(core, []).append((waits, transfers))
        for _, sem, dsts, part in transfers:
            ne = NE if part is None else NE // 2
            for d, _ in dsts:
                assert topo.may_write(core, d) and d != core
                expect[(d, sem)] = expect.get((d, sem), 0) + ne
            expect[(core, "sent")] = expect.get((core, "sent"), 0) + ne

    for s in ranks:
        b = idx[s]
        a = "a%d" % b
        q = cabled(s)
        g_own, g_near = gate(twin(s), True), gate(twin(near(s)), False)
        expect[(s, a)] = 16
        expect[(s, "ldd")] = 16
        add(s, ["ldd"], [(None, "fed", [(g_near, None), (g_own, None)], 1)])
        add(s, [], [(None, a, [(q, b)], 0), (None, a, [(near(s), b)], 1)])
        add(g_near, ["fed"], [(None, a, [(twin(near(q)), b)], 0), (None, a, [(twin(near(s)), b)], 1)])
        add(g_own, ["fed"], [(None, a, [(twin(q), b)], 0), (None, a, [(twin(s), b)], 1)])
    for s in ranks:
        b = idx[cabled(s)]
        add(s, ["a%d" % b], [(b, "a%d" % b, [(near(s), b)], None)])
    return calls, expect


def _remote(g, core, T, topo, call, expect):
    waits, transfers = call

    def ap(where):
        return T.hold[:, :] if where is None else T.win[:, where * W:(where + 1) * W]

    for name in waits:
        g.wait_ge(T.sem[name], expect[(core, name)])
    out = []
    for src, sem, dsts, part in transfers:
        mask = topo.mask(core, dsts[0][0])
        ids = []
        for d, _ in dsts:
            mask &= topo.mask(core, d)
            rid, pid = topo.addr(d, core)
            ids.append(DstId(rid=rid, pnc=pid))
        out.append(RemoteDMATransfer(dst_ids=ids, dma_engine_mask=_engines(mask, part), remote_sem=T.sem[sem],
                                     srcs=[ap(src)], dsts=[ap(where) for _, where in dsts]))
    g.remote_dma_fused(out, local_sem=T.sem.sent)


def rank_program(g, core, T, topo):
    if "plan" not in _CACHE:
        _CACHE["plan"] = _plan(list(T.cores), topo)
    calls, expect = _CACHE["plan"]
    mine = calls.get(core, [])
    rank = T.rank_of(core)
    if rank is None:
        for call in mine:
            _remote(g, core, T, topo, call, expect)
        if mine:
            g.wait_ge(T.sem.sent, expect[(core, "sent")])
        return

    sem, v, act, add, mult = T.sem, g.vector, g.scalar, AluOpType.add, AluOpType.mult
    own = T.win[:, rank * W:(rank + 1) * W]

    g.sync.dma_start(out=T.hold[:, :], in_=T.x[:, :]).then_inc(sem.ldd, 16)
    act.dma_start(out=T.lnrow[0:1, 0:16], in_=T.ln[0:8, :]).then_inc(sem.lnl, 16)
    act.dma_start(out=own, in_=T.x[:, :]).then_inc(sem["a%d" % rank], 16)

    g.iota(T.pm[:, 0:1], [[0, 1]], 0, 1).then_inc(sem.gi, 1)
    g.iota(T.c16[:, :], [[16, 64]], 0, 0, allow_small_or_imprecise_dtypes=True).then_inc(sem.gi, 1)
    g.iota(T.c16w[:, :], [[0, NP], [16, 64 // NP]], 0, 0,
           allow_small_or_imprecise_dtypes=True).then_inc(sem.gi, 1)
    for call in mine[0:2]:
        _remote(g, core, T, topo, call, expect)
    g.wait_ge(sem.lnl, 16)
    g.partition_broadcast(T.lnb[:, :], T.lnrow[0:1, 0:16], 128).then_inc(sem.gb, 1)
    for call in mine[2:]:
        _remote(g, core, T, topo, call, expect)
    g.wait_ge(sem.sent, expect[(core, "sent")])

    n = [0]

    def done(inst):
        inst.then_inc(sem.vs, 1)
        n[0] += 1

    def bar():
        v.wait_ge(sem.vs, n[0])

    v.memset(T.win[:, ZC:ZC + 4], 0.0).then_inc(sem.zs, 1)
    done(v.memset(T.zer[:, :], 0.0))
    v.wait_ge(sem.gi, 3)
    done(v.tensor_scalar(out=T.pm[:, 0:1], in0=T.pm[:, 0:1], scalar1=15, scalar2=None, op0=AluOpType.bitwise_and))
    bar()
    done(v.tensor_copy(out=T.pmf[:, 0:1], in_=T.pm[:, 0:1]))
    bar()
    done(v.tensor_scalar(out=T.jj[:, :], in0=T.c16[:, :], scalar1=T.pmf[:, 0:1], scalar2=None, op0=add))
    done(v.tensor_scalar(out=T.jw[:, :], in0=T.c16w[:, :], scalar1=T.pmf[:, 0:1], scalar2=None, op0=add))
    v.wait_ge(sem.gb, 1)
    done(v.tensor_copy(out=T.lnf[:, :], in_=T.lnb[:, 0:16:2]))
    bar()
    done(v.tensor_tensor_scan(out=T.cum[:, :], data0=T.lnf[:, :], data1=T.zer[:, :], initial=0.0, op0=add, op1=add))
    done(v.tensor_scalar(out=T.gap[:, :], in0=T.lnf[:, :], scalar1=-1.0, scalar2=float(W), op0=mult, op1=add))
    bar()
    for r in range(N):
        done(v.tensor_scalar(out=T.tmp[:, 64 * r:64 * (r + 1)], in0=T.jj[:, :], scalar1=T.cum[:, r:r + 1],
                             scalar2=T.gap[:, r:r + 1], op0=AluOpType.is_ge, op1=mult))
    bar()
    h = 64 * N // 2
    while h >= 64:
        done(v.tensor_tensor(out=T.tmp[:, 0:h], in0=T.tmp[:, 0:h], in1=T.tmp[:, h:2 * h], op=add))
        bar()
        h //= 2
    done(v.tensor_tensor(out=T.tmp[:, 0:64], in0=T.tmp[:, 0:64], in1=T.jw[:, :], op=add))
    bar()
    k = 64 // NP
    for q in range(NP):
        v.tensor_scalar(out=T.off[:, q * k:(q + 1) * k], in0=T.tmp[:, q * k:(q + 1) * k], scalar1=float(ZC - q * PW),
                        scalar2=None, op0=AluOpType.min).then_inc(sem.offr, 1)

    for eng in (v, act):
        eng.wait_ge(sem.offr, NP)
        eng.wait_ge(sem.zs, 1)
    seen = {0: N, 1: N}
    for q in range(NP - 1, -1, -1):
        e = q % 2
        eng = act if e else v
        first = q * PW // W
        for b in range(seen[e] - 1, first - 1, -1):
            eng.wait_ge(sem["a%d" % b], expect[(core, "a%d" % b)])
        seen[e] = first
        src = T.win[:, q * PW:ZC + 4].indirect(T.off[:, q * k:(q + 1) * k])
        dst = T.outb[:, q * PW:(q + 1) * PW]
        if e:
            act.activation(out=dst, in_=src, func=ActivationFunctionType.Copy).then_inc(sem["p%d" % q], 1)
        else:
            v.tensor_copy(out=dst, in_=src).then_inc(sem["p%d" % q], 1)

    for q in range(NP - 2, -1, -2):
        g.sync.wait_ge(sem["p%d" % (q + 1)], 1)
        g.sync.wait_ge(sem["p%d" % q], 1)
        g.sync.dma_start(out=T.y[:, q * PW:(q + 2) * PW], in_=T.outb[:, q * PW:(q + 2) * PW]).then_inc(sem.sts, 16)
    g.sync.wait_ge(sem.sts, 16 * (NP // 2))
